import numpy as np
import ml_dtypes


def mxq(x, axis, fmt="e4m3"):
    dtype, down = {"e4m3": (ml_dtypes.float8_e4m3fn, 7), "e5m2": (ml_dtypes.float8_e5m2, 14)}[fmt]
    v = np.moveaxis(np.asarray(x, np.float32).astype(ml_dtypes.bfloat16).astype(np.float64), axis, -1)
    blocks = v.reshape(v.shape[:-1] + (-1, 32))
    amax = np.abs(blocks).max(-1, keepdims=True)
    byte = np.maximum(np.where(amax > 0, np.frexp(amax)[1] - 1 + 127, 0) - down, 1)
    scale = np.exp2(byte - 127.0)
    codes = (blocks / scale).astype(np.float32).astype(dtype).astype(np.float64)
    return np.moveaxis((codes * scale).reshape(v.shape), -1, axis)


WIDE = False


def mx_kscale(k):
    if not WIDE:
        return np.ones(k)
    levels = np.array([10, -10, 5, -5, 0])
    if k % 512:
        return np.exp2(np.random.permutation(np.resize(levels, k // 32))).repeat(32)
    a = np.empty((k // 512, 16))
    for p in range(k // 512):
        a[p, :8] = np.random.permutation(np.resize(levels, 8))
        for g in range(8):
            far = levels[np.abs(levels - a[p, g]) >= 10]
            a[p, g + 8] = far[np.random.randint(len(far))]
    return np.exp2(a.ravel()).repeat(32)


def f64(x):
    return np.asarray(x).astype(np.float64)


def striped(idx):
    return np.tile(idx.reshape(-1, 16).T, (8, 1)).astype(np.uint16)


def unstriped(offs):
    return offs[:16].T.reshape(-1).astype(np.int64)


def striped8(idx):
    return np.concatenate([x.reshape(-1, 16).T for x in idx]).astype(np.uint16)


def runs(offs, k):
    lists = np.stack([offs[16 * r : 16 * r + 16].T.reshape(-1) for r in range(8)]).astype(np.int64)
    return lists[np.arange(k) % 512 // 64]


def pack_weight(w):
    k, n = w.shape
    w = f64(np.asarray(w, np.float32).astype(ml_dtypes.bfloat16)).reshape(k // 32, 32, n)
    amax = np.abs(w).max(1)
    byte = np.clip(np.where(amax > 0, np.frexp(amax)[1] - 1 + 127 - 7, 1), 1, 254)
    scaled = (w * np.exp2(127.0 - byte)[:, None, :]).reshape(k, n).astype(np.float32)
    words = np.ascontiguousarray(scaled.reshape(k // 512, 128, 4, n).transpose(0, 1, 3, 2)).astype(ml_dtypes.float8_e4m3fn).view(np.uint8)
    return words, np.ascontiguousarray(byte.astype(np.uint8).reshape(k // 512, 16, n))


def unpack_weight(words, scales):
    g, p, n, _ = words.shape
    vals = np.ascontiguousarray(words).view(ml_dtypes.float8_e4m3fn).astype(np.float64) * np.repeat(np.exp2(scales.astype(np.float64) - 127.0), 8, axis=1)[..., None]
    return vals.transpose(0, 1, 3, 2).reshape(g * 512, n)


K, T, S, N, H, W = 512, 2048, 512, 512, 512, 256


def setup_inputs():
    n = np.random.standard_normal
    s = mx_kscale(K)[:, None]
    u = mx_kscale(S)
    packed_xT = pack_weight(n((K, T)) * s)
    perm = np.stack([np.random.permutation(H) for _ in range(8)])
    return {
        "x_words": packed_xT[0],
        "x_scales": packed_xT[1],
        "wa": (n((K, H)) / np.sqrt(K) / s).astype(np.float32),
        "gt": (np.random.uniform(0.5, 1.5, (S, 1)) * u[:, None]).astype(np.float32),
        "w1": (n((S, N)) / np.sqrt(S) / u[:, None]).astype(np.float32),
        "offs": striped(np.random.permutation(T)[:S]),
        "n1": striped8(np.stack([np.random.permutation(H) for _ in range(8)])),
        "n2": striped8(np.stack([np.random.permutation(H) for _ in range(8)])),
        "n3": striped8(perm[:, :W]),
        "n4": striped8(perm[:, W:]),
    }


def reference(x_words, x_scales, wa, gt, w1, offs, n1, n2, n3, n4):
    xq = unpack_weight(x_words, x_scales)[:, unstriped(offs)]
    y = xq.T @ mxq(f64(wa), 0, "e4m3")
    z = f64(gt) * ((y[np.arange(S)[:, None], runs(n1, S)]) * (y[np.arange(S)[:, None], runs(n2, S)]))
    h = mxq(f64(w1), 0, "e4m3").T @ mxq(z, 0, "e4m3")
    pb = h[np.arange(N)[:, None], runs(n4, N)]
    pa = h[np.arange(N)[:, None], runs(n3, N)]
    rb = pb - (0.5 * pa)
    ra = np.sqrt((pa) ** 2 + (pb) ** 2 + 0.25)
    ds = np.zeros((N, H))
    ds[np.arange(N)[:, None], runs(n3, N)] = ra
    out = ds.copy()
    out[np.arange(N)[:, None], runs(n4, N)] = rb
    return out

@@ -1,0 +1,229 @@
+from contextlib import ExitStack
+
+import concourse.mybir as mybir
+
+K, T, S, N, H, W = 512, 2048, 512, 512, 512, 256
+FLOPS = 2 * K * S * H + 2 * S * N * H
+
+F32 = mybir.dt.float32
+BF16 = mybir.dt.bfloat16
+I32 = mybir.dt.int32
+U32 = mybir.dt.uint32
+U16 = mybir.dt.uint16
+U8 = mybir.dt.uint8
+FP8X4 = mybir.dt.float8_e4m3fn_x4
+ACT = mybir.ActivationFunctionType
+ALU = mybir.AluOpType
+
+P = 128
+PACK = 4
+HALF = 256
+LINE = 4
+WA_VECTOR_COLS = 128
+
+
+def tile_picked_tokprodpolar_none_p_kernel(
+    tc, x_words, x_scales, wa, gt, w1, offs, n1, n2, n3, n4, out
+):
+    nc = tc.nc
+    with ExitStack() as ctx:
+        keep = ctx.enter_context(tc.tile_pool(name="keep", bufs=1))
+        reused = ctx.enter_context(tc.tile_pool(name="reused", bufs=1))
+        psum = ctx.enter_context(tc.psum_pool(name="psum", bufs=1))
+
+        def sbuf(shape, dtype, name):
+            return keep.tile(shape, dtype, name=name, align_bytes=64)
+
+        offs_sb = keep.tile([P, S // 16], U16, name="offs_sb")
+        n1_sb = keep.tile([P, H // 16], U16, name="n1_sb")
+        n2_sb = keep.tile([P, H // 16], U16, name="n2_sb")
+        n3_sb = keep.tile([P, W // 16], U16, name="n3_sb")
+        n4_sb = keep.tile([P, W // 16], U16, name="n4_sb")
+        words_all = sbuf([P, T], U32, "words_all")
+        scales_all = sbuf([P, T], U8, "scales_all")
+        wa_raw = [
+            sbuf([P, PACK, HALF], F32, "wa_raw0"),
+            reused.tile([P, PACK, HALF], F32, name="wa_raw1", offset=0, align_bytes=64),
+        ]
+        w1_raw = sbuf([P, PACK, N], F32, "w1_raw")
+        gt_sb = sbuf([P, PACK], F32, "gt_sb")
+
+        nc.vector.memset(scales_all[:].bitcast(I32), 0)
+        nc.sync.dma_start(offs_sb[:], offs)
+        wa_rows = wa.rearrange("(p j) c -> p j c", j=PACK)
+        nc.sync.dma_start(wa_raw[0][:], wa_rows[:, :, :HALF])
+        for q in range(4):
+            nc.sync.dma_start(
+                scales_all[32 * q : 32 * q + 4, :].bitcast(I32), x_scales[0, 4 * q : 4 * q + 4, :].bitcast(I32)
+            )
+        nc.sync.dma_start(words_all[:].bitcast(I32), x_words[0].rearrange("p c r -> p (c r)").bitcast(I32))
+        nc.sync.dma_start(wa_raw[1][:], wa_rows[:, :, HALF:])
+        nc.sync.dma_start(n1_sb[:], n1)
+        nc.sync.dma_start(n2_sb[:], n2)
+        nc.sync.dma_start(w1_raw[:], w1.rearrange("(p j) c -> p j c", j=PACK))
+        nc.sync.dma_start(gt_sb[:], gt.rearrange("(p j) o -> p (j o)", j=PACK))
+        nc.sync.dma_start(n3_sb[:], n3)
+        nc.sync.dma_start(n4_sb[:], n4)
+
+        scales_picked = sbuf([P, S], U8, "scales_picked")
+        x_scale = sbuf([P, PACK, P], U8, "x_scale")
+        x_code = sbuf([P, PACK, P], U32, "x_code")
+        wa_code = sbuf([P, H], U32, "wa_code")
+        wa_scale = sbuf([P, H], U8, "wa_scale")
+        wa_bf = [
+            sbuf([P, HALF, PACK], BF16, "wa_bf0"),
+            reused.tile([P, HALF, PACK], BF16, name="wa_bf1", offset=5120, align_bytes=64),
+        ]
+        halves = [slice(h * HALF, (h + 1) * HALF) for h in range(2)]
+
+        def interleave_wa(copy, h, c0, c1):
+            copy(
+                wa_bf[h][:, c0:c1, :].rearrange("p (c i) j -> p c j i", i=LINE),
+                wa_raw[h][:, :, c0:c1].rearrange("p j (c i) -> p c j i", i=LINE),
+            )
+
+        def quantize(code, scale, values):
+            nc.vector.quantize_mx(out=code.bitcast(FP8X4), scales=scale, in_=values)
+
+        def quantize_wa(h):
+            quantize(wa_code[:, halves[h]], wa_scale[:, halves[h]], wa_bf[h][:].rearrange("p c j -> p (c j)"))
+
+        def product_mx(bank, code, scale, t, rhs_code, rhs_scale, cols):
+            acc = psum.tile([P, cols.stop - cols.start], F32, name="acc", tag="bank%d" % bank)
+            nc.tensor.matmul_mx(
+                out=acc[:],
+                lhsT=code[:, t, :].bitcast(FP8X4),
+                lhsT_scale=scale[:, t, :],
+                rhs=rhs_code[:, cols].bitcast(FP8X4),
+                rhs_scale=rhs_scale[:, cols],
+                start=True,
+                stop=True,
+            )
+            return acc
+
+        interleave_wa(nc.scalar.copy, 0, 0, HALF)
+        nc.vector.tensor_copy(scales_picked[:], scales_all[:].indirect(offs_sb[:]))
+        quantize_wa(0)
+        nc.vector.tensor_copy(x_scale[:], scales_picked[:].rearrange("p (m t) -> p t m", t=PACK))
+        nc.vector.tensor_copy(x_code[:].rearrange("p t m -> p m t"), words_all[:].indirect(offs_sb[:]))
+        interleave_wa(nc.vector.tensor_copy, 1, 0, WA_VECTOR_COLS)
+        interleave_wa(nc.scalar.copy, 1, WA_VECTOR_COLS, HALF)
+        quantize_wa(1)
+
+        y_sb = [reused.tile([P, H], F32, name="y_sb%d" % t, offset=2048 * t, align_bytes=64) for t in range(PACK)]
+        on_scalar = [(0, 0), (0, 1), (1, 0), (1, 3)]
+
+        def make_y(h, t):
+            acc = product_mx(PACK * h + t, x_code, x_scale, t, wa_code, wa_scale, halves[h])
+            copy = nc.scalar.copy if (h, t) in on_scalar else nc.vector.tensor_copy
+            return lambda: copy(y_sb[t][:, halves[h]], acc[:])
+
+        y_out = {(h, t): make_y(h, t) for h in range(2) for t in range(PACK)}
+        for t in range(PACK):
+            y_out[0, t]()
+        for t in range(PACK - 1):
+            y_out[1, t]()
+
+        z_code = sbuf([P, H], U32, "z_code")
+        z_scale = sbuf([P, H], U8, "z_scale")
+        prods = [sbuf([P, PACK, HALF], F32, "prod%d" % h) for h in range(2)]
+        z_bf = [sbuf([P, HALF, PACK], BF16, "z_bf%d" % h) for h in range(2)]
+
+        def product(h, t):
+            entries = slice(h * HALF // 16, (h + 1) * HALF // 16)
+            first = keep.tile([P, HALF], F32, name="first", tag="first%d%d" % (h, t), align_bytes=64)
+            nc.scalar.activation(first[:], y_sb[t][:].indirect(n1_sb[:, entries]), ACT.Copy)
+            nc.vector.tensor_tensor(prods[h][:, t, :], y_sb[t][:].indirect(n2_sb[:, entries]), first[:], ALU.mult)
+
+        def weigh(h):
+            nc.vector.tensor_tensor(
+                z_bf[h][:].rearrange("p (c i) t -> p c t i", i=LINE),
+                prods[h][:].rearrange("p t (c i) -> p c t i", i=LINE),
+                gt_sb[:].unsqueeze(1).unsqueeze(3).to_broadcast([P, HALF // LINE, PACK, LINE]),
+                ALU.mult,
+            )
+
+        def quantize_z(h):
+            cols = slice(h * HALF, (h + 1) * HALF)
+            quantize(z_code[:, cols], z_scale[:, cols], z_bf[h][:].rearrange("p c t -> p (c t)"))
+
+        w1_code = sbuf([P, PACK, P], U32, "w1_code")
+        w1_scale = sbuf([P, PACK, P], U8, "w1_scale")
+        w1_bf = {}
+
+        def interleave_w1(u, tag):
+            w1_bf[u] = keep.tile([P, 2, P, PACK], BF16, name="w1_bf", tag=tag, align_bytes=64)
+            nc.scalar.copy(
+                w1_bf[u][:].rearrange("p t m j -> p m j t"),
+                w1_raw[:].rearrange("p j (m t) -> p m j t", t=PACK)[:, :, :, 2 * u : 2 * u + 2],
+            )
+
+        def quantize_w1(u):
+            quantize(
+                w1_code[:, 2 * u : 2 * u + 2, :].rearrange("p t m -> p (t m)"),
+                w1_scale[:, 2 * u : 2 * u + 2, :].rearrange("p t m -> p (t m)"),
+                w1_bf[u][:].rearrange("p t m j -> p (t m j)"),
+            )
+
+        h_sb = [sbuf([P, H], F32, "h_sb%d" % t) for t in range(PACK)]
+
+        def make_h(t, bank, cols):
+            acc = product_mx(bank, w1_code, w1_scale, t, z_code, z_scale, cols)
+            nc.scalar.copy(h_sb[t][:, cols], acc[:])
+
+        for t in range(PACK):
+            if t == PACK - 1:
+                y_out[1, t]()
+            product(0, t)
+        product(1, 0)
+        weigh(0)
+        interleave_w1(0, "first03")
+        product(1, 1)
+        quantize_z(0)
+        product(1, 2)
+        quantize_w1(0)
+        product(1, 3)
+        interleave_w1(1, "first11")
+        make_h(0, 0, halves[0])
+        make_h(1, 1, halves[0])
+        weigh(1)
+        quantize_w1(1)
+        quantize_z(1)
+
+        pair = [sbuf([P, 2, W], F32, "pair%d" % t) for t in range(PACK)]
+        total = [sbuf([P, W], F32, "total%d" % t) for t in range(PACK)]
+        res = [sbuf([P, H], F32, "res%d" % t) for t in range(PACK)]
+        out_rows = out.rearrange("(p t) c -> t p c", t=PACK)
+
+        def fetch(t):
+            if t < 2:
+                make_h(t, PACK + t, halves[1])
+            else:
+                make_h(t, t, slice(0, H))
+            nc.scalar.activation(pair[t][:, 0, :], h_sb[t][:].indirect(n3_sb[:]), ACT.Copy, scale=-0.5)
+            if t == 0:
+                nc.vector.tensor_copy(pair[t][:, 1, :], h_sb[t][:].indirect(n4_sb[:]))
+            else:
+                nc.scalar.activation(pair[t][:, 1, :], h_sb[t][:].indirect(n4_sb[:]), ACT.Copy)
+
+        def put_rb(t):
+            nc.vector.tensor_tensor(res[t][:].indirect(n4_sb[:]), pair[t][:, 1, :], pair[t][:, 0, :], ALU.add)
+
+        def add_squares(t):
+            squares = sbuf([P, 2, W], F32, "squares%d" % t)
+            nc.scalar.activation(squares[:], pair[t][:], ACT.Square)
+            nc.vector.scalar_tensor_tensor(total[t][:], squares[:, 0, :], 4.0, squares[:, 1, :], ALU.mult, ALU.add)
+
+        def put_ra(t):
+            ra = sbuf([P, W], F32, "ra%d" % t)
+            nc.scalar.activation(ra[:], total[t][:], ACT.Sqrt, bias=0.25)
+            nc.vector.tensor_copy(res[t][:].indirect(n3_sb[:]), ra[:])
+            nc.sync.dma_start(out_rows[t], res[t][:])
+
+        for t in range(PACK):
+            fetch(t)
+            put_rb(t)
+            add_squares(t)
+            if t > 0:
+                put_ra(t - 1)
+        put_ra(PACK - 1)

@@ -40,7 +40,7 @@ def tile_picked_tokprodpolar_none_p_kernel(
         n3_sb = keep.tile([P, W // 16], U16, name="n3_sb")
         n4_sb = keep.tile([P, W // 16], U16, name="n4_sb")
         words_all = sbuf([P, T], U32, "words_all")
-        scales_all = sbuf([P, T], U8, "scales_all")
+        scales_all = keep.tile([P, T], U8, name="scales_all", tag="scales_all", align_bytes=64)
         wa_raw = [
             sbuf([P, PACK, HALF], F32, "wa_raw0"),
             reused.tile([P, PACK, HALF], F32, name="wa_raw1", offset=0, align_bytes=64),
@@ -49,6 +49,9 @@ def tile_picked_tokprodpolar_none_p_kernel(
         gt_sb = sbuf([P, PACK], F32, "gt_sb")
 
         nc.vector.memset(scales_all[:].bitcast(I32), 0)
+        warm = sbuf([P, 2], F32, "warm")
+        nc.vector.memset(warm[:, 0:1], 1.0)
+        nc.scalar.activation(warm[:, 1:2], warm[:, 0:1], ACT.Sqrt)
         nc.sync.dma_start(offs_sb[:], offs)
         wa_rows = wa.rearrange("(p j) c -> p j c", j=PACK)
         nc.sync.dma_start(wa_raw[0][:], wa_rows[:, :, :HALF])
@@ -68,8 +71,11 @@ def tile_picked_tokprodpolar_none_p_kernel(
         scales_picked = sbuf([P, S], U8, "scales_picked")
         x_scale = sbuf([P, PACK, P], U8, "x_scale")
         x_code = sbuf([P, PACK, P], U32, "x_code")
-        wa_code = sbuf([P, H], U32, "wa_code")
-        wa_scale = sbuf([P, H], U8, "wa_scale")
+        wa_code = [
+            keep.tile([P, HALF], U32, name="wa_code0", tag="scales_all", align_bytes=64),
+            sbuf([P, HALF], U32, "wa_code1"),
+        ]
+        wa_scale = [sbuf([P, HALF], U8, "wa_scale%d" % h) for h in range(2)]
         wa_bf = [
             sbuf([P, HALF, PACK], BF16, "wa_bf0"),
             reused.tile([P, HALF, PACK], BF16, name="wa_bf1", offset=5120, align_bytes=64),
@@ -86,16 +92,16 @@ def tile_picked_tokprodpolar_none_p_kernel(
             nc.vector.quantize_mx(out=code.bitcast(FP8X4), scales=scale, in_=values)
 
         def quantize_wa(h):
-            quantize(wa_code[:, halves[h]], wa_scale[:, halves[h]], wa_bf[h][:].rearrange("p c j -> p (c j)"))
+            quantize(wa_code[h][:], wa_scale[h][:], wa_bf[h][:].rearrange("p c j -> p (c j)"))
 
-        def product_mx(bank, code, scale, t, rhs_code, rhs_scale, cols):
-            acc = psum.tile([P, cols.stop - cols.start], F32, name="acc", tag="bank%d" % bank)
+        def product_mx(bank, code, scale, t, rhs_code, rhs_scale):
+            acc = psum.tile([P, rhs_scale.shape[1]], F32, name="acc", tag="bank%d" % bank)
             nc.tensor.matmul_mx(
                 out=acc[:],
                 lhsT=code[:, t, :].bitcast(FP8X4),
                 lhsT_scale=scale[:, t, :],
-                rhs=rhs_code[:, cols].bitcast(FP8X4),
-                rhs_scale=rhs_scale[:, cols],
+                rhs=rhs_code.bitcast(FP8X4),
+                rhs_scale=rhs_scale,
                 start=True,
                 stop=True,
             )
@@ -111,29 +117,45 @@ def tile_picked_tokprodpolar_none_p_kernel(
         quantize_wa(1)
 
         y_sb = [reused.tile([P, H], F32, name="y_sb%d" % t, offset=2048 * t, align_bytes=64) for t in range(PACK)]
-        on_scalar = [(0, 0), (0, 1), (1, 0), (1, 3)]
+        def make_y(copy, t, bank, h):
+            acc = product_mx(bank, x_code, x_scale, t, wa_code[h][:], wa_scale[h][:])
+            copy(y_sb[t][:, halves[h]], acc[:])
 
-        def make_y(h, t):
-            acc = product_mx(PACK * h + t, x_code, x_scale, t, wa_code, wa_scale, halves[h])
-            copy = nc.scalar.copy if (h, t) in on_scalar else nc.vector.tensor_copy
-            return lambda: copy(y_sb[t][:, halves[h]], acc[:])
-
-        y_out = {(h, t): make_y(h, t) for h in range(2) for t in range(PACK)}
-        for t in range(PACK):
-            y_out[0, t]()
-        for t in range(PACK - 1):
-            y_out[1, t]()
+        make_y(nc.scalar.copy, 0, 0, 0)
+        make_y(nc.scalar.copy, 1, 1, 0)
+        make_y(nc.vector.tensor_copy, 2, 2, 0)
+        make_y(nc.scalar.copy, 0, 4, 1)
+        make_y(nc.vector.tensor_copy, 1, 5, 1)
+        make_y(nc.vector.tensor_copy, 3, 2, 0)
+        make_y(nc.vector.tensor_copy, 2, 6, 1)
+        make_y(nc.vector.tensor_copy, 3, 3, 1)
 
         z_code = sbuf([P, H], U32, "z_code")
         z_scale = sbuf([P, H], U8, "z_scale")
         prods = [sbuf([P, PACK, HALF], F32, "prod%d" % h) for h in range(2)]
-        z_bf = [sbuf([P, HALF, PACK], BF16, "z_bf%d" % h) for h in range(2)]
+        z_bf = [keep.tile([P, HALF, PACK], BF16, name="z_bf", tag="z_bf%d" % h, align_bytes=64) for h in range(2)]
 
         def product(h, t):
             entries = slice(h * HALF // 16, (h + 1) * HALF // 16)
             first = keep.tile([P, HALF], F32, name="first", tag="first%d%d" % (h, t), align_bytes=64)
             nc.scalar.activation(first[:], y_sb[t][:].indirect(n1_sb[:, entries]), ACT.Copy)
             nc.vector.tensor_tensor(prods[h][:, t, :], y_sb[t][:].indirect(n2_sb[:, entries]), first[:], ALU.mult)
+
+        def look_up_both(h, t, both):
+            entries = slice(h * HALF // 16, (h + 1) * HALF // 16)
+            nc.scalar.activation(both[:, 0, :], y_sb[t][:].indirect(n1_sb[:, entries]), ACT.Copy)
+            nc.scalar.activation(both[:, 1, :], y_sb[t][:].indirect(n2_sb[:, entries]), ACT.Copy)
+
+        def weighed_product(t, both):
+            nc.vector.scalar_tensor_tensor(
+                z_rows[:, t, :], both[:, 0, :], gt_sb[:, t : t + 1], both[:, 1, :], ALU.mult, ALU.mult
+            )
+
+        def interleave_z(h):
+            nc.vector.tensor_copy(
+                z_bf[h][:].rearrange("p (c i) t -> p c t i", i=LINE),
+                z_rows[:].rearrange("p t (c i) -> p c t i", i=LINE),
+            )
 
         def weigh(h):
             nc.vector.tensor_tensor(
@@ -147,48 +169,55 @@ def tile_picked_tokprodpolar_none_p_kernel(
             cols = slice(h * HALF, (h + 1) * HALF)
             quantize(z_code[:, cols], z_scale[:, cols], z_bf[h][:].rearrange("p c t -> p (c t)"))
 
-        w1_code = sbuf([P, PACK, P], U32, "w1_code")
-        w1_scale = sbuf([P, PACK, P], U8, "w1_scale")
+        w1_code = {}
+        w1_scale = [sbuf([P, 2, P], U8, "w1_scale%d" % u) for u in range(2)]
         w1_bf = {}
 
-        def interleave_w1(u, tag):
+        def interleave_w1(copy, u, tag):
             w1_bf[u] = keep.tile([P, 2, P, PACK], BF16, name="w1_bf", tag=tag, align_bytes=64)
-            nc.scalar.copy(
+            copy(
                 w1_bf[u][:].rearrange("p t m j -> p m j t"),
                 w1_raw[:].rearrange("p j (m t) -> p m j t", t=PACK)[:, :, :, 2 * u : 2 * u + 2],
             )
 
-        def quantize_w1(u):
+        def quantize_w1(u, tag):
+            w1_code[u] = keep.tile([P, 2, P], U32, name="w1_code", tag=tag, align_bytes=64)
             quantize(
-                w1_code[:, 2 * u : 2 * u + 2, :].rearrange("p t m -> p (t m)"),
-                w1_scale[:, 2 * u : 2 * u + 2, :].rearrange("p t m -> p (t m)"),
+                w1_code[u][:].rearrange("p t m -> p (t m)"),
+                w1_scale[u][:].rearrange("p t m -> p (t m)"),
                 w1_bf[u][:].rearrange("p t m j -> p (t m j)"),
             )
 
-        h_sb = [sbuf([P, H], F32, "h_sb%d" % t) for t in range(PACK)]
+        h_sb = [keep.tile([P, H], F32, name="h_sb", tag="h_sb%d" % t, align_bytes=64) for t in range(PACK)]
 
         def make_h(t, bank, cols):
-            acc = product_mx(bank, w1_code, w1_scale, t, z_code, z_scale, cols)
+            acc = product_mx(bank, w1_code[t // 2], w1_scale[t // 2], t % 2, z_code[:, cols], z_scale[:, cols])
             nc.scalar.copy(h_sb[t][:, cols], acc[:])
 
+        both0 = sbuf([P, 2, HALF], F32, "both0")
+        look_up_both(1, 0, both0)
+        interleave_w1(nc.vector.tensor_copy, 0, "w1_bf0")
         for t in range(PACK):
-            if t == PACK - 1:
-                y_out[1, t]()
             product(0, t)
-        product(1, 0)
+        z_rows = keep.tile([P, PACK, HALF], BF16, name="z_rows", tag="first00", align_bytes=64)
+        both1 = keep.tile([P, 2, HALF], F32, name="both1", tag="first01", align_bytes=64)
+        both23 = keep.tile([P, 2, 2, HALF], F32, name="both23", tag="first02", align_bytes=64)
+        look_up_both(1, 1, both1)
+        look_up_both(1, 2, both23[:, 0, :, :])
+        look_up_both(1, 3, both23[:, 1, :, :])
         weigh(0)
-        interleave_w1(0, "first03")
-        product(1, 1)
+        weighed_product(0, both0)
         quantize_z(0)
-        product(1, 2)
-        quantize_w1(0)
-        product(1, 3)
-        interleave_w1(1, "first11")
+        quantize_w1(0, "first03")
+        weighed_product(1, both1)
+        weighed_product(2, both23[:, 0, :, :])
+        weighed_product(3, both23[:, 1, :, :])
         make_h(0, 0, halves[0])
         make_h(1, 1, halves[0])
-        weigh(1)
-        quantize_w1(1)
+        interleave_w1(nc.scalar.copy, 1, "first01")
+        interleave_z(1)
         quantize_z(1)
+        quantize_w1(1, "z_bf1")
 
         pair = [sbuf([P, 2, W], F32, "pair%d" % t) for t in range(PACK)]
         total = [sbuf([P, W], F32, "total%d" % t) for t in range(PACK)]
@@ -215,7 +244,7 @@ def tile_picked_tokprodpolar_none_p_kernel(
             nc.vector.scalar_tensor_tensor(total[t][:], squares[:, 0, :], 4.0, squares[:, 1, :], ALU.mult, ALU.add)
 
         def put_ra(t):
-            ra = sbuf([P, W], F32, "ra%d" % t)
+            ra = keep.tile([P, W], F32, name="ra", tag="h_sb%d" % ((t + 1) % PACK), align_bytes=64)
             nc.scalar.activation(ra[:], total[t][:], ACT.Sqrt, bias=0.25)
             nc.vector.tensor_copy(res[t][:].indirect(n3_sb[:]), ra[:])
             nc.sync.dma_start(out_rows[t], res[t][:])

@@ -70,7 +70,7 @@ def tile_picked_tokprodpolar_none_p_kernel(
 
         scales_picked = sbuf([P, S], U8, "scales_picked")
         x_scale = sbuf([P, PACK, P], U8, "x_scale")
-        x_code = sbuf([P, PACK, P], U32, "x_code")
+        x_code = keep.tile([P, PACK, P], U32, name="x_code", tag="x_code", align_bytes=64)
         wa_code = [
             keep.tile([P, HALF], U32, name="wa_code0", tag="scales_all", align_bytes=64),
             sbuf([P, HALF], U32, "wa_code1"),
@@ -133,7 +133,11 @@ def tile_picked_tokprodpolar_none_p_kernel(
         z_code = sbuf([P, H], U32, "z_code")
         z_scale = sbuf([P, H], U8, "z_scale")
         prods = [sbuf([P, PACK, HALF], F32, "prod%d" % h) for h in range(2)]
-        z_bf = [keep.tile([P, HALF, PACK], BF16, name="z_bf", tag="z_bf%d" % h, align_bytes=64) for h in range(2)]
+        pieces = [slice(0, HALF), slice(HALF, HALF + P), slice(HALF + P, H)]
+        z_bf = [
+            keep.tile([P, c.stop - c.start, PACK], BF16, name="z_bf", tag="z_bf%d" % i, align_bytes=64)
+            for i, c in enumerate(pieces)
+        ]
 
         def product(h, t):
             entries = slice(h * HALF // 16, (h + 1) * HALF // 16)
@@ -141,20 +145,21 @@ def tile_picked_tokprodpolar_none_p_kernel(
             nc.scalar.activation(first[:], y_sb[t][:].indirect(n1_sb[:, entries]), ACT.Copy)
             nc.vector.tensor_tensor(prods[h][:, t, :], y_sb[t][:].indirect(n2_sb[:, entries]), first[:], ALU.mult)
 
-        def look_up_both(h, t, both):
-            entries = slice(h * HALF // 16, (h + 1) * HALF // 16)
-            nc.scalar.activation(both[:, 0, :], y_sb[t][:].indirect(n1_sb[:, entries]), ACT.Copy)
-            nc.scalar.activation(both[:, 1, :], y_sb[t][:].indirect(n2_sb[:, entries]), ACT.Copy)
+        def look_up_both(t, both, c0, c1):
+            entries = slice((HALF + c0) // 16, (HALF + c1) // 16)
+            nc.scalar.activation(both[:, 0, c0:c1], y_sb[t][:].indirect(n1_sb[:, entries]), ACT.Copy)
+            nc.scalar.activation(both[:, 1, c0:c1], y_sb[t][:].indirect(n2_sb[:, entries]), ACT.Copy)
 
-        def weighed_product(t, both):
+        def weighed_product(t, both, c0, c1):
             nc.vector.scalar_tensor_tensor(
-                z_rows[:, t, :], both[:, 0, :], gt_sb[:, t : t + 1], both[:, 1, :], ALU.mult, ALU.mult
+                z_rows[:, t, c0:c1], both[:, 0, c0:c1], gt_sb[:, t : t + 1], both[:, 1, c0:c1], ALU.mult, ALU.mult
             )
 
-        def interleave_z(h):
+        def interleave_z(i):
+            cols = slice(pieces[i].start - HALF, pieces[i].stop - HALF)
             nc.vector.tensor_copy(
-                z_bf[h][:].rearrange("p (c i) t -> p c t i", i=LINE),
-                z_rows[:].rearrange("p t (c i) -> p c t i", i=LINE),
+                z_bf[i][:].rearrange("p (c i) t -> p c t i", i=LINE),
+                z_rows[:, :, cols].rearrange("p t (c i) -> p c t i", i=LINE),
             )
 
         def weigh(h):
@@ -166,7 +171,7 @@ def tile_picked_tokprodpolar_none_p_kernel(
             )
 
         def quantize_z(h):
-            cols = slice(h * HALF, (h + 1) * HALF)
+            cols = pieces[h]
             quantize(z_code[:, cols], z_scale[:, cols], z_bf[h][:].rearrange("p c t -> p (c t)"))
 
         w1_code = {}
@@ -195,40 +200,46 @@ def tile_picked_tokprodpolar_none_p_kernel(
             nc.scalar.copy(h_sb[t][:, cols], acc[:])
 
         both0 = sbuf([P, 2, HALF], F32, "both0")
-        look_up_both(1, 0, both0)
-        interleave_w1(nc.vector.tensor_copy, 0, "w1_bf0")
+        look_up_both(0, both0, 0, HALF)
+        interleave_w1(nc.vector.tensor_copy, 0, "x_code")
+        quantize_w1(0, "w1_code0")
         for t in range(PACK):
             product(0, t)
         z_rows = keep.tile([P, PACK, HALF], BF16, name="z_rows", tag="first00", align_bytes=64)
         both1 = keep.tile([P, 2, HALF], F32, name="both1", tag="first01", align_bytes=64)
         both23 = keep.tile([P, 2, 2, HALF], F32, name="both23", tag="first02", align_bytes=64)
-        look_up_both(1, 1, both1)
-        look_up_both(1, 2, both23[:, 0, :, :])
-        look_up_both(1, 3, both23[:, 1, :, :])
+        both2, both3 = both23[:, 0, :, :], both23[:, 1, :, :]
+        look_up_both(1, both1, 0, HALF)
+        look_up_both(2, both2, 0, HALF)
+        look_up_both(3, both3, 0, P)
+        look_up_both(3, both3, P, HALF)
         weigh(0)
-        weighed_product(0, both0)
+        weighed_product(0, both0, 0, HALF)
         quantize_z(0)
-        quantize_w1(0, "first03")
-        weighed_product(1, both1)
-        weighed_product(2, both23[:, 0, :, :])
-        weighed_product(3, both23[:, 1, :, :])
-        make_h(0, 0, halves[0])
-        make_h(1, 1, halves[0])
-        interleave_w1(nc.scalar.copy, 1, "first01")
+        weighed_product(1, both1, 0, HALF)
+        weighed_product(2, both2, 0, HALF)
+        weighed_product(3, both3, 0, P)
+        make_h(0, 0, pieces[0])
+        make_h(1, 1, pieces[0])
         interleave_z(1)
+        weighed_product(3, both3, P, HALF)
         quantize_z(1)
-        quantize_w1(1, "z_bf1")
+        make_h(0, 7, pieces[1])
+        interleave_z(2)
+        quantize_z(2)
+        interleave_w1(nc.vector.tensor_copy, 1, "z_bf2")
+        quantize_w1(1, "w1_code1")
 
-        pair = [sbuf([P, 2, W], F32, "pair%d" % t) for t in range(PACK)]
-        total = [sbuf([P, W], F32, "total%d" % t) for t in range(PACK)]
+        pair = [keep.tile([P, 2, W], F32, name="pair", tag="pair%d" % t, align_bytes=64) for t in range(PACK)]
+        total = {}
         res = [sbuf([P, H], F32, "res%d" % t) for t in range(PACK)]
         out_rows = out.rearrange("(p t) c -> t p c", t=PACK)
 
         def fetch(t):
-            if t < 2:
-                make_h(t, PACK + t, halves[1])
-            else:
-                make_h(t, t, slice(0, H))
+            if t == 0:
+                make_h(0, 4, pieces[2])
+            if t >= 2:
+                make_h(t, 5, slice(0, H))
             nc.scalar.activation(pair[t][:, 0, :], h_sb[t][:].indirect(n3_sb[:]), ACT.Copy, scale=-0.5)
             if t == 0:
                 nc.vector.tensor_copy(pair[t][:, 1, :], h_sb[t][:].indirect(n4_sb[:]))
@@ -240,8 +251,11 @@ def tile_picked_tokprodpolar_none_p_kernel(
 
         def add_squares(t):
             squares = sbuf([P, 2, W], F32, "squares%d" % t)
-            nc.scalar.activation(squares[:], pair[t][:], ACT.Square)
-            nc.vector.scalar_tensor_tensor(total[t][:], squares[:, 0, :], 4.0, squares[:, 1, :], ALU.mult, ALU.add)
+            nc.scalar.activation(squares[:, 0, :], pair[t][:, 0, :], ACT.Square, scale=2.0)
+            nc.scalar.activation(squares[:, 1, :], pair[t][:, 1, :], ACT.Square)
+            total[t] = keep.tile([P, W], F32, name="total", tag="pair%d" % t if t else "total0", align_bytes=64)
+            add = nc.vector.tensor_tensor if t == 0 else nc.gpsimd.tensor_tensor
+            add(total[t][:], squares[:, 0, :], squares[:, 1, :], ALU.add)
 
         def put_ra(t):
             ra = keep.tile([P, W], F32, name="ra", tag="h_sb%d" % ((t + 1) % PACK), align_bytes=64)
@@ -252,6 +266,8 @@ def tile_picked_tokprodpolar_none_p_kernel(
         for t in range(PACK):
             fetch(t)
             put_rb(t)
+            if t == 0:
+                make_h(1, 5, halves[1])
             add_squares(t)
             if t > 0:
                 put_ra(t - 1)

from contextlib import ExitStack

import concourse.mybir as mybir

K, T, S, N, H, W = 512, 2048, 512, 512, 512, 256
FLOPS = 2 * K * S * H + 2 * S * N * H

F32 = mybir.dt.float32
BF16 = mybir.dt.bfloat16
I32 = mybir.dt.int32
U32 = mybir.dt.uint32
U16 = mybir.dt.uint16
U8 = mybir.dt.uint8
FP8X4 = mybir.dt.float8_e4m3fn_x4
ACT = mybir.ActivationFunctionType
ALU = mybir.AluOpType

P = 128
PACK = 4
HALF = 256
LINE = 4
WA_VECTOR_COLS = 128


def tile_picked_tokprodpolar_none_p_kernel(
    tc, x_words, x_scales, wa, gt, w1, offs, n1, n2, n3, n4, out
):
    nc = tc.nc
    with ExitStack() as ctx:
        keep = ctx.enter_context(tc.tile_pool(name="keep", bufs=1))
        reused = ctx.enter_context(tc.tile_pool(name="reused", bufs=1))
        psum = ctx.enter_context(tc.psum_pool(name="psum", bufs=1))

        def sbuf(shape, dtype, name):
            return keep.tile(shape, dtype, name=name, align_bytes=64)

        offs_sb = keep.tile([P, S // 16], U16, name="offs_sb")
        n1_sb = keep.tile([P, H // 16], U16, name="n1_sb")
        n2_sb = keep.tile([P, H // 16], U16, name="n2_sb")
        n3_sb = keep.tile([P, W // 16], U16, name="n3_sb")
        n4_sb = keep.tile([P, W // 16], U16, name="n4_sb")
        words_all = sbuf([P, T], U32, "words_all")
        scales_all = keep.tile([P, T], U8, name="scales_all", tag="scales_all", align_bytes=64)
        wa_raw = [
            sbuf([P, PACK, HALF], F32, "wa_raw0"),
            reused.tile([P, PACK, HALF], F32, name="wa_raw1", offset=0, align_bytes=64),
        ]
        w1_raw = sbuf([P, PACK, N], F32, "w1_raw")
        gt_sb = sbuf([P, PACK], F32, "gt_sb")

        nc.vector.memset(scales_all[:].bitcast(I32), 0)
        warm = sbuf([P, 2], F32, "warm")
        nc.vector.memset(warm[:, 0:1], 1.0)
        nc.scalar.activation(warm[:, 1:2], warm[:, 0:1], ACT.Sqrt)
        nc.sync.dma_start(offs_sb[:], offs)
        wa_rows = wa.rearrange("(p j) c -> p j c", j=PACK)
        nc.sync.dma_start(wa_raw[0][:], wa_rows[:, :, :HALF])
        for q in range(4):
            nc.sync.dma_start(
                scales_all[32 * q : 32 * q + 4, :].bitcast(I32), x_scales[0, 4 * q : 4 * q + 4, :].bitcast(I32)
            )
        nc.sync.dma_start(words_all[:].bitcast(I32), x_words[0].rearrange("p c r -> p (c r)").bitcast(I32))
        nc.sync.dma_start(wa_raw[1][:], wa_rows[:, :, HALF:])
        nc.sync.dma_start(n1_sb[:], n1)
        nc.sync.dma_start(n2_sb[:], n2)
        nc.sync.dma_start(w1_raw[:], w1.rearrange("(p j) c -> p j c", j=PACK))
        nc.sync.dma_start(gt_sb[:], gt.rearrange("(p j) o -> p (j o)", j=PACK))
        nc.sync.dma_start(n3_sb[:], n3)
        nc.sync.dma_start(n4_sb[:], n4)

        scales_picked = sbuf([P, S], U8, "scales_picked")
        x_scale = sbuf([P, PACK, P], U8, "x_scale")
        x_code = keep.tile([P, PACK, P], U32, name="x_code", tag="x_code", align_bytes=64)
        wa_code = [
            keep.tile([P, HALF], U32, name="wa_code0", tag="scales_all", align_bytes=64),
            sbuf([P, HALF], U32, "wa_code1"),
        ]
        wa_scale = [sbuf([P, HALF], U8, "wa_scale%d" % h) for h in range(2)]
        wa_bf = [
            sbuf([P, HALF, PACK], BF16, "wa_bf0"),
            reused.tile([P, HALF, PACK], BF16, name="wa_bf1", offset=5120, align_bytes=64),
        ]
        halves = [slice(h * HALF, (h + 1) * HALF) for h in range(2)]

        def interleave_wa(copy, h, c0, c1):
            copy(
                wa_bf[h][:, c0:c1, :].rearrange("p (c i) j -> p c j i", i=LINE),
                wa_raw[h][:, :, c0:c1].rearrange("p j (c i) -> p c j i", i=LINE),
            )

        def quantize(code, scale, values):
            nc.vector.quantize_mx(out=code.bitcast(FP8X4), scales=scale, in_=values)

        def quantize_wa(h):
            quantize(wa_code[h][:], wa_scale[h][:], wa_bf[h][:].rearrange("p c j -> p (c j)"))

        def product_mx(bank, code, scale, t, rhs_code, rhs_scale):
            acc = psum.tile([P, rhs_scale.shape[1]], F32, name="acc", tag="bank%d" % bank)
            nc.tensor.matmul_mx(
                out=acc[:],
                lhsT=code[:, t, :].bitcast(FP8X4),
                lhsT_scale=scale[:, t, :],
                rhs=rhs_code.bitcast(FP8X4),
                rhs_scale=rhs_scale,
                start=True,
                stop=True,
            )
            return acc

        interleave_wa(nc.scalar.copy, 0, 0, HALF)
        nc.vector.tensor_copy(scales_picked[:], scales_all[:].indirect(offs_sb[:]))
        quantize_wa(0)
        nc.vector.tensor_copy(x_scale[:], scales_picked[:].rearrange("p (m t) -> p t m", t=PACK))
        nc.vector.tensor_copy(x_code[:].rearrange("p t m -> p m t"), words_all[:].indirect(offs_sb[:]))
        interleave_wa(nc.vector.tensor_copy, 1, 0, WA_VECTOR_COLS)
        interleave_wa(nc.scalar.copy, 1, WA_VECTOR_COLS, HALF)
        quantize_wa(1)

        y_sb = [reused.tile([P, H], F32, name="y_sb%d" % t, offset=2048 * t, align_bytes=64) for t in range(PACK)]
        def make_y(copy, t, bank, h):
            acc = product_mx(bank, x_code, x_scale, t, wa_code[h][:], wa_scale[h][:])
            copy(y_sb[t][:, halves[h]], acc[:])

        make_y(nc.scalar.copy, 0, 0, 0)
        make_y(nc.scalar.copy, 1, 1, 0)
        make_y(nc.vector.tensor_copy, 2, 2, 0)
        make_y(nc.scalar.copy, 0, 4, 1)
        make_y(nc.vector.tensor_copy, 1, 5, 1)
        make_y(nc.vector.tensor_copy, 3, 2, 0)
        make_y(nc.vector.tensor_copy, 2, 6, 1)
        make_y(nc.vector.tensor_copy, 3, 3, 1)

        z_code = sbuf([P, H], U32, "z_code")
        z_scale = sbuf([P, H], U8, "z_scale")
        prods = [sbuf([P, PACK, HALF], F32, "prod%d" % h) for h in range(2)]
        pieces = [slice(0, HALF), slice(HALF, HALF + P), slice(HALF + P, H)]
        z_bf = [
            keep.tile([P, c.stop - c.start, PACK], BF16, name="z_bf", tag="z_bf%d" % i, align_bytes=64)
            for i, c in enumerate(pieces)
        ]

        def product(h, t):
            entries = slice(h * HALF // 16, (h + 1) * HALF // 16)
            first = keep.tile([P, HALF], F32, name="first", tag="first%d%d" % (h, t), align_bytes=64)
            nc.scalar.activation(first[:], y_sb[t][:].indirect(n1_sb[:, entries]), ACT.Copy)
            nc.vector.tensor_tensor(prods[h][:, t, :], y_sb[t][:].indirect(n2_sb[:, entries]), first[:], ALU.mult)

        def look_up_both(t, both, c0, c1):
            entries = slice((HALF + c0) // 16, (HALF + c1) // 16)
            nc.scalar.activation(both[:, 0, c0:c1], y_sb[t][:].indirect(n1_sb[:, entries]), ACT.Copy)
            nc.scalar.activation(both[:, 1, c0:c1], y_sb[t][:].indirect(n2_sb[:, entries]), ACT.Copy)

        def weighed_product(t, both, c0, c1):
            nc.vector.scalar_tensor_tensor(
                z_rows[:, t, c0:c1], both[:, 0, c0:c1], gt_sb[:, t : t + 1], both[:, 1, c0:c1], ALU.mult, ALU.mult
            )

        def interleave_z(i):
            cols = slice(pieces[i].start - HALF, pieces[i].stop - HALF)
            nc.vector.tensor_copy(
                z_bf[i][:].rearrange("p (c i) t -> p c t i", i=LINE),
                z_rows[:, :, cols].rearrange("p t (c i) -> p c t i", i=LINE),
            )

        def weigh(h):
            nc.vector.tensor_tensor(
                z_bf[h][:].rearrange("p (c i) t -> p c t i", i=LINE),
                prods[h][:].rearrange("p t (c i) -> p c t i", i=LINE),
                gt_sb[:].unsqueeze(1).unsqueeze(3).to_broadcast([P, HALF // LINE, PACK, LINE]),
                ALU.mult,
            )

        def quantize_z(h):
            cols = pieces[h]
            quantize(z_code[:, cols], z_scale[:, cols], z_bf[h][:].rearrange("p c t -> p (c t)"))

        w1_code = {}
        w1_scale = [sbuf([P, 2, P], U8, "w1_scale%d" % u) for u in range(2)]
        w1_bf = {}

        def interleave_w1(copy, u, tag):
            w1_bf[u] = keep.tile([P, 2, P, PACK], BF16, name="w1_bf", tag=tag, align_bytes=64)
            copy(
                w1_bf[u][:].rearrange("p t m j -> p m j t"),
                w1_raw[:].rearrange("p j (m t) -> p m j t", t=PACK)[:, :, :, 2 * u : 2 * u + 2],
            )

        def quantize_w1(u, tag):
            w1_code[u] = keep.tile([P, 2, P], U32, name="w1_code", tag=tag, align_bytes=64)
            quantize(
                w1_code[u][:].rearrange("p t m -> p (t m)"),
                w1_scale[u][:].rearrange("p t m -> p (t m)"),
                w1_bf[u][:].rearrange("p t m j -> p (t m j)"),
            )

        h_sb = [keep.tile([P, H], F32, name="h_sb", tag="h_sb%d" % t, align_bytes=64) for t in range(PACK)]

        def make_h(t, bank, cols):
            acc = product_mx(bank, w1_code[t // 2], w1_scale[t // 2], t % 2, z_code[:, cols], z_scale[:, cols])
            nc.scalar.copy(h_sb[t][:, cols], acc[:])

        both0 = sbuf([P, 2, HALF], F32, "both0")
        look_up_both(0, both0, 0, HALF)
        interleave_w1(nc.vector.tensor_copy, 0, "x_code")
        quantize_w1(0, "w1_code0")
        for t in range(PACK):
            product(0, t)
        z_rows = keep.tile([P, PACK, HALF], BF16, name="z_rows", tag="first00", align_bytes=64)
        both1 = keep.tile([P, 2, HALF], F32, name="both1", tag="first01", align_bytes=64)
        both23 = keep.tile([P, 2, 2, HALF], F32, name="both23", tag="first02", align_bytes=64)
        both2, both3 = both23[:, 0, :, :], both23[:, 1, :, :]
        look_up_both(1, both1, 0, HALF)
        look_up_both(2, both2, 0, HALF)
        look_up_both(3, both3, 0, P)
        look_up_both(3, both3, P, HALF)
        weigh(0)
        weighed_product(0, both0, 0, HALF)
        quantize_z(0)
        weighed_product(1, both1, 0, HALF)
        weighed_product(2, both2, 0, HALF)
        weighed_product(3, both3, 0, P)
        make_h(0, 0, pieces[0])
        make_h(1, 1, pieces[0])
        interleave_z(1)
        weighed_product(3, both3, P, HALF)
        quantize_z(1)
        make_h(0, 7, pieces[1])
        interleave_z(2)
        quantize_z(2)
        interleave_w1(nc.vector.tensor_copy, 1, "z_bf2")
        quantize_w1(1, "w1_code1")

        pair = [keep.tile([P, 2, W], F32, name="pair", tag="pair%d" % t, align_bytes=64) for t in range(PACK)]
        total = {}
        res = [sbuf([P, H], F32, "res%d" % t) for t in range(PACK)]
        out_rows = out.rearrange("(p t) c -> t p c", t=PACK)

        def fetch(t):
            if t == 0:
                make_h(0, 4, pieces[2])
            if t >= 2:
                make_h(t, 5, slice(0, H))
            nc.scalar.activation(pair[t][:, 0, :], h_sb[t][:].indirect(n3_sb[:]), ACT.Copy, scale=-0.5)
            if t == 0:
                nc.vector.tensor_copy(pair[t][:, 1, :], h_sb[t][:].indirect(n4_sb[:]))
            else:
                nc.scalar.activation(pair[t][:, 1, :], h_sb[t][:].indirect(n4_sb[:]), ACT.Copy)

        def put_rb(t):
            nc.vector.tensor_tensor(res[t][:].indirect(n4_sb[:]), pair[t][:, 1, :], pair[t][:, 0, :], ALU.add)

        def add_squares(t):
            squares = sbuf([P, 2, W], F32, "squares%d" % t)
            nc.scalar.activation(squares[:, 0, :], pair[t][:, 0, :], ACT.Square, scale=2.0)
            nc.scalar.activation(squares[:, 1, :], pair[t][:, 1, :], ACT.Square)
            total[t] = keep.tile([P, W], F32, name="total", tag="pair%d" % t if t else "total0", align_bytes=64)
            add = nc.vector.tensor_tensor if t == 0 else nc.gpsimd.tensor_tensor
            add(total[t][:], squares[:, 0, :], squares[:, 1, :], ALU.add)

        def put_ra(t):
            ra = keep.tile([P, W], F32, name="ra", tag="h_sb%d" % ((t + 1) % PACK), align_bytes=64)
            nc.scalar.activation(ra[:], total[t][:], ACT.Sqrt, bias=0.25)
            nc.vector.tensor_copy(res[t][:].indirect(n3_sb[:]), ra[:])
            nc.sync.dma_start(out_rows[t], res[t][:])

        for t in range(PACK):
            fetch(t)
            put_rb(t)
            if t == 0:
                make_h(1, 5, halves[1])
            add_squares(t)
            if t > 0:
                put_ra(t - 1)
        put_ra(PACK - 1)
